import numpy as np, ml_dtypes
CORES = [8,136,40,168]
N = 4
BF = ml_dtypes.bfloat16
def f(rng, *shape):
    return (rng.standard_normal(shape, dtype=np.float32) * np.exp2(rng.integers(-2, 3, shape[:-1] + (1,)))).astype(BF)
def wide(rng, *shape):
    v = f(rng, *shape).astype(np.float32); k = shape[:-2] + (1, shape[-1])
    return (v * np.exp2(rng.integers(-6, 7, k)) * (rng.random(k) > 0.0625)).astype(BF)
def gentries(a):
    return np.ascontiguousarray(a.reshape(8, 16, -1).transpose(0, 2, 1)).reshape(8, -1)
def gtable(e):
    e = np.asarray(e); return np.ascontiguousarray(e.reshape(8, -1, 16).transpose(0, 2, 1)).reshape(128, -1).astype(np.int32)
E, D, CAP, S, P = 4096, 4, 256, 2, 5120
def setup_inputs(rng):
    mp = rng.integers(0, 8, (8, S)); mp[:, S - 1] = rng.permutation(8); i, j = rng.permutation(8)[:2]; mp[j, :S - 1] = mp[i, :S - 1]
    sh = (N, 8, D * E); pl = np.where(rng.random(sh) < 0.5, rng.integers(0, E, sh), rng.integers(E, P, sh)); se = rng.integers(0, E, (N, 8, N * CAP))
    return {"x": f(rng, N, 16, E), "mp": np.repeat(mp[None], N, 0).astype(np.int32),
            "src": np.stack([gtable(e) for e in pl]), "snd": np.stack([gtable(e) for e in se]),
            "bs": f(rng, N, 128, 1).astype(np.float32) * np.float32(0.25),
            "aw": rng.standard_normal((N, 16, 16), dtype=np.float32) * np.float32(0.5),
            "ab": rng.standard_normal((N, 16, 1), dtype=np.float32) * np.float32(0.25),
            "aq": np.clip(0.4 * rng.standard_normal((N, 16, 1)), -1, 1).astype(np.float32)}
def setup_inputs_full(rng):
    d = setup_inputs(rng)
    d["src"] = np.stack([gtable(np.stack([E + rng.permutation(D * E) % (N * CAP) for k in range(8)])) for r in range(N)])
    d["snd"] = np.stack([gtable(np.stack([np.concatenate([rng.permutation(E)[:CAP] for q in range(N)]) for k in range(8)])) for r in range(N)]); return d
def setup_inputs_edges(rng):
    d = setup_inputs(rng); ends = np.array([0, E - 1] + [E + q * CAP + i for q in range(N) for i in (0, CAP - 1)])
    pl = rng.choice(ends, (N, 8, D * E)); pl[:, rng.integers(0, 8)] = P - 1; se = rng.choice(np.array([0, E - 1]), (N, 8, N * CAP))
    d["src"] = np.stack([gtable(e) for e in pl]); d["snd"] = np.stack([gtable(e) for e in se]); return d
def setup_inputs_chains(rng):
    d = setup_inputs(rng); c = rng.choice(np.array([0, 7]), (3, S)); c[1, 0] = 0; c[2, 0] = 7; c[:, S - 1] = rng.permutation(8)[:3]; c[0] = c[0, S - 1]
    d["mp"] = np.repeat(c[rng.permutation(np.array([0, 0, 0, 1, 1, 2, 2, 2]))][None], N, 0).astype(np.int32); return d
def setup_inputs_dead(rng):
    d = setup_inputs(rng); k, z = rng.permutation(8)[:2]; d["bs"][:, 16 * k:16 * k + 16] = -4096; d["bs"][:, 16 * z:16 * z + 16] = 0
    g = int(np.flatnonzero(d["mp"][0, :, S - 1] != k)[rng.integers(0, 7)]); d["mp"][:, g, 0] = k; return d
def setup_inputs_spread(rng):
    d = setup_inputs(rng); d["x"] = wide(rng, N, 16, E); return d
def check_inputs(d):
    bad = []
    for a, n in (("src", P), ("snd", E), ("mp", 8)):
        if d[a].min() < 0 or d[a].max() >= n: bad.append("range of " + a)
    if (d["mp"] != d["mp"][:1]).any(): bad.append("mp is the same on all ranks")
    if not (np.abs(d["aq"]) <= 1).all(): bad.append("range of aq")
    for a in ("x", "bs", "aw", "ab", "aq"):
        if not np.isfinite(d[a].astype(np.float32)).all(): bad.append("finite " + a)
    return bad
def reference(x, mp, src, snd, bs, aw, ab, aq):
    h = np.repeat(x.astype(np.float64)[:, None], 8, axis=1)
    pl = np.stack([gentries(a) for a in src]); se = np.stack([gentries(a) for a in snd]).reshape(N, 8, N, CAP); b = bs.astype(np.float64).reshape(N, 8, 16, 1)
    for s in range(S):
        nh = np.zeros_like(h)
        for g in range(8):
            k = int(mp[0, g, s])
            for r in range(N):
                win = np.concatenate([h[r, g]] + [h[q, g][:, se[q, k, r]] for q in range(N)], axis=1)
                v = np.sum(win[:, pl[r, k]].reshape(16, D, E), axis=1)
                nh[r, g] = np.maximum(v * 2.0 ** -2 + b[r, k], 0)
        h = nh
    tot = np.zeros(8, np.float64)
    for r in range(N):
        for g in range(8):
            t = np.tanh(aw[r].astype(np.float64).T @ h[r, g] + ab[r].astype(np.float64))
            tot[g] += np.sum(aq[r].astype(np.float64) * t)
    w = np.exp(tot * 2.0 ** -14)
    y = np.einsum("g,rgce->rce", w, h)
    return {"y": y.astype(np.float32), "w": np.repeat(w[None, :, None], N, axis=0).astype(np.float32)}

@@ -1,0 +1,334 @@
+from concourse.bass import DstId, RemoteDMATransfer, IndirectOffsetOnAxis
+from concourse.mybir import AluOpType, AxisListType, ActivationFunctionType
+
+E, CAP, N = 4096, 256, 4
+P = E + N * CAP
+SCRATCH = {"aqd": ("dram", [128, 1], "float32"), "aql": ("dram", [4, 128, 1], "float32"),
+           "ps": ("psum", [128, 4096], "float32")}
+for _rows, _cols, _dt, _names in (
+        (128, 128, "bfloat16", "onesb permb"), (8, 128, "bfloat16", "c16 r16a r16 mpr0 mpr1"), (16, 128, "bfloat16", "lb"),
+        (16, 128, "float32", "l32 awr"), (128, 128, "float32", "cn ones bda bd perm0 perm1 awb q0 q1 q2 q3"),
+        (128, 1, "int32", "pio pm"), (128, 1, "float32", "pmf bst b0 b1 abc so st eo et wv"), (8, 2, "int32", "mpi"),
+        (8, 2, "bfloat16", "mpf"), (8, 2, "float32", "mpg"), (128, 2, "int32", "idx"), (16, 1, "float32", "abt"),
+        (16, E, "bfloat16", "xs"), (128, 64, "int32", "snd0i snd1i"), (128, 64, "uint16", "snd0 snd1"),
+        (128, 1024, "int32", "l0i l1i"), (128, 1024, "uint16", "l0 l1"), (128, P, "bfloat16", "w0"), (128, P, "float32", "w1"),
+        (128, 3 * CAP, "bfloat16", "sb0"), (128, 3 * CAP, "float32", "sb1"), (128, E, "bfloat16", "ga gb gg gd th"),
+        (128, E, "float32", "a0 a1 h"), (128, 48, "float32", "acc"), (128, 16, "float32", "aqs d16 wm"),
+        (128, 512, "float32", "yt")):
+    for _n in _names.split():
+        SCRATCH[_n] = ("sbuf", [_rows, _cols], _dt)
+SEMAPHORES = ["cV", "cS", "cP", "cG", "dx", "dsnd", "dmp", "dsrc", "daq", "dbs", "daw", "dql", "gi", "st0", "st1", "dw",
+              "aqa", "arr0", "arr1", "sca", "loc"]
+
+
+def rank_program(g, core, T, topo):
+    r = T.rank_of(core)
+    if r is None:
+        return
+    A, F = AluOpType, ActivationFunctionType
+    queues = {"V": g.vector, "S": g.scalar, "P": g.tensor, "G": g, "Y": g.sync}
+    cnt = {"V": 0, "S": 0, "P": 0, "G": 0}
+    seen = {}
+    total = {}
+
+    def wait(q, *tokens):
+        for t in tokens:
+            s, v = t
+            if seen.get((q, s), 0) < v:
+                queues[q].wait_ge(T.sem[s], v)
+                seen[(q, s)] = v
+
+    def done(q, ins):
+        ins.then_inc(T.sem["c" + q], 1)
+        cnt[q] += 1
+        return ("c" + q, cnt[q])
+
+    def dma(q, sem, out, in_):
+        queues[q].dma_start(out, in_).then_inc(T.sem[sem], 16)
+        total[sem] = total.get(sem, 0) + 16
+        return (sem, total[sem])
+
+    peers = [T.cores[(r + k) % N] for k in (1, 2, 3)]
+    ranks = [(r + k) % N for k in (1, 2, 3)]
+    eng = len(topo.engines(core, peers[0]))
+    nloc = [0]
+
+    def send(out, in_, sem, dst):
+        rid, pid = topo.addr(dst, core)
+        g.remote_dma(out, in_, T.sem[sem], T.sem.loc, pid, rid, topo.mask(core, dst))
+        nloc[0] += len(topo.engines(core, dst))
+
+    def send_all(out, in_, sem):
+        ids = []
+        for d in peers:
+            rid, pid = topo.addr(d, core)
+            ids.append(DstId(rid=rid, pnc=pid))
+        g.remote_dma_fused([RemoteDMATransfer(dst_ids=ids, dma_engine_mask=topo.mask(core, peers[0]),
+                                              remote_sem=T.sem[sem], src=in_, dsts=[out, out, out])], local_sem=T.sem.loc)
+        nloc[0] += eng
+
+    def bank(b, n, o=0):
+        return T.ps[:, 512 * b + o:512 * b + o + n]
+
+    def gather(q, out, win, off, deps):
+        wait(q, *deps)
+        if q == "V":
+            return done("V", g.vector.tensor_copy(out, win.indirect(off)))
+        return done("S", g.scalar.activation(out, win.indirect(off), F.Identity))
+
+    tx = dma("Y", "dx", T.xs[:], T.x[:])
+    tsnd = dma("S", "dsnd", T.snd0i[:], T.snd[:])
+    tmp = dma("S", "dmp", T.mpi[:], T.mp[:])
+    for k in range(8):
+        taq = dma("S", "daq", T.aqd[16 * k:16 * k + 16, :], T.aq[:])
+    tsrc = dma("Y", "dsrc", T.l0i[:], T.src[:])
+    tbs = dma("Y", "dbs", T.bst[:], T.bs[:])
+    dma("Y", "daw", T.abt[:], T.ab[:])
+    for k in range(8):
+        taw = dma("Y", "daw", T.awr[:, 16 * k:16 * k + 16], T.aw[:])
+
+    v1 = done("V", g.vector.memset(T.onesb[:], 1.0))
+    v2 = done("V", g.vector.memset(T.c16[:], 16.0))
+    v3 = done("V", g.vector.memset(T.ones[:], 1.0))
+    wait("G", v1)
+    tlb = done("G", g.affine_select(T.lb[:], T.onesb[0:16, :], [[0, 8], [1, 16]], A.is_equal, 0.0, 0, -1))
+    wait("G", v2)
+    t = done("G", g.affine_select(T.r16a[:], T.c16[:], [[1, 128]], A.is_ge, 0.0, 0, -16))
+    wait("G", t)
+    tr16 = done("G", g.affine_select(T.r16[:], T.r16a[:], [[-1, 128]], A.is_ge, 0.0, 15, 16))
+    tpio = done("G", g.iota(T.pio[:], [[0, 1]], 0, 1))
+    wait("G", taq)
+    send_all(T.aql[r], T.aqd[:], "aqa")
+    tcn = done("G", g.iota(T.cn[:], [[0, 8], [-1, 16]], 0, 1, allow_small_or_imprecise_dtypes=True))
+    wait("G", v3)
+    t = done("G", g.affine_select(T.bda[:], T.ones[:], [[-16, 8], [0, 16]], A.is_ge, 0.0, 0, 1))
+    wait("G", t)
+    tbd = done("G", g.affine_select(T.bd[:], T.bda[:], [[16, 8], [0, 16]], A.is_ge, 0.0, 15, -1))
+
+    wait("P", tlb, tx)
+    px = [done("P", g.tensor.matmul(bank(b, 512), T.lb[:], T.xs[:, 512 * b:512 * b + 512], True, True)) for b in range(8)]
+    wait("V", tsnd)
+    vsnd = done("V", g.vector.tensor_copy(T.snd0[:], T.snd0i[:]))
+    xe = []
+    for b in range(8):
+        q = "VS"[b % 2]
+        wait(q, px[b])
+        o = T.w0[:, 512 * b:512 * b + 512]
+        if q == "V":
+            xe.append(done("V", g.vector.tensor_copy(o, bank(b, 512))))
+        else:
+            xe.append(done("S", g.scalar.activation(o, bank(b, 512), F.Identity)))
+
+    def exchange(win, sb, lists, deps, sem):
+        w = win[:, 0:E]
+        tk = []
+        for i, q in ((0, "V"), (1, "S"), (2, "V")):
+            off = lists[:, 16 * ranks[i]:16 * ranks[i] + 16]
+            tk.append(gather(q, sb[:, CAP * i:CAP * i + CAP], w, off, deps))
+        own = gather("S", win[:, E + CAP * r:E + CAP * r + CAP], w, lists[:, 16 * r:16 * r + 16], deps)
+        for i in range(3):
+            wait("G", tk[i])
+            send(win[:, E + CAP * r:E + CAP * r + CAP], sb[:, CAP * i:CAP * i + CAP], sem, peers[i])
+        return own
+
+    own0 = exchange(T.w0, T.sb0, T.snd0, xe + [vsnd], "arr0")
+
+    wait("V", tmp)
+    t = done("V", g.vector.tensor_copy(T.mpf[:], T.mpi[:]))
+    t3 = done("V", g.vector.tensor_copy(T.mpg[:], T.mpi[:]))
+    wait("V", tpio)
+    t2 = done("V", g.vector.tensor_scalar(T.pm[:], T.pio[:], 15, None, A.bitwise_and))
+    wait("V", t3)
+    tm = [done("V", g.vector.tensor_scalar(T.mpr0[:], T.onesb[0:8, :], T.mpg[:, 0:1], None, A.mult)),
+          done("V", g.vector.tensor_scalar(T.mpr1[:], T.onesb[0:8, :], T.mpg[:, 1:2], None, A.mult))]
+    wait("V", t2)
+    tpm = done("V", g.vector.tensor_copy(T.pmf[:], T.pm[:]))
+    wait("P", tr16, *tm)
+    wait("P", *xe)
+    pidx = done("P", g.tensor.matmul(bank(2, 2), T.r16[:], T.mpf[:], True, True))
+    pa = [done("P", g.tensor.matmul(bank(s, 128), (T.mpr0, T.mpr1)[s][:], T.r16[:], True, True)) for s in (0, 1)]
+    wait("V", pidx, tpm)
+    tidx = done("V", g.vector.tensor_scalar(T.idx[:], bank(2, 2), T.pmf[:], None, A.add))
+    wait("V", tcn, *pa)
+    tp = [done("V", g.vector.tensor_tensor((T.perm0, T.perm1)[s][:], bank(s, 128), T.cn[:], A.is_equal)) for s in (0, 1)]
+    wait("V", tsrc)
+    vl0 = done("V", g.vector.tensor_copy(T.l0[:], T.l0i[:]))
+    wait("V", tp[0])
+    tpb = done("V", g.vector.tensor_scalar(T.permb[:], T.perm0[:], 0.0625, None, A.mult))
+    wait("P", tbs, *tp)
+    pb = [done("P", g.tensor.matmul(bank(3 + s, 1), (T.perm0, T.perm1)[s][:], T.bst[:], True, True)) for s in (0, 1)]
+    wait("V", *pb)
+    tb0 = done("V", g.vector.tensor_scalar(T.b0[:], bank(3, 1), 0.25, None, A.mult))
+    tb1 = done("V", g.vector.tensor_copy(T.b1[:], bank(4, 1)))
+    wait("G", tidx)
+    for o, tab in ((T.snd1i, T.snd), (T.l1i, T.src)):
+        g.indirect_dma_start(o[:], None, tab[:], IndirectOffsetOnAxis(ap=T.idx[:, 1:2], axis=0),
+                             bounds_check=127).then_inc(T.sem.gi, 16)
+    wait("Y", taq)
+    dma("Y", "dql", T.aqs[:, 4 * r:4 * r + 1], T.aqd[:])
+    wait("Y", ("aqa", 3 * eng))
+    for q in ranks:
+        tql = dma("Y", "dql", T.aqs[:, 4 * q:4 * q + 1], T.aql[q])
+
+    bufs = (T.ga, T.gb, T.gg, T.gd)
+    chunks = [(0, 1024), (1024, 1024), (2048, 1024), (3072, 512), (3584, 256), (3840, 256)]
+    arrived = [("arr0", 3 * eng), own0, vl0] + xe
+    pend, h0, npiece = [], [], 0
+
+    def evac(p):
+        e0, n, b, q, tk = p
+        o, i = T.w1[:, e0:e0 + n], bank(b, n)
+        wait(q, tk, tb0)
+        if q == "V":
+            h0.append(done("V", g.vector.tensor_scalar(o, i, T.b0[:], 0.0, A.add, A.max)))
+        else:
+            h0.append(done("S", g.scalar.activation(o, i, F.Relu, bias=T.b0[:])))
+
+    for e0, n in chunks:
+        tk = [gather("VVSS"[d], bufs[d][:, e0:e0 + n], T.w0[:],
+                     T.l0[:, 256 * d + e0 // 16:256 * d + (e0 + n) // 16], arrived) for d in (0, 2, 1, 3)]
+        for p in pend:
+            evac(p)
+        pend = []
+        for c0 in range(e0, e0 + n, 512):
+            m = min(512, e0 + n - c0)
+            b = npiece % 8
+            wait("P", tpb, tb0, tb1)
+            if npiece >= 8:
+                wait("P", h0[npiece - 8])
+            for i, d in enumerate((0, 2, 1, 3)):
+                wait("P", tk[i])
+                x = done("P", g.tensor.matmul(bank(b, m), T.permb[:], bufs[d][:, c0:c0 + m], i == 0, i == 3))
+            pend.append((c0, m, b, "VS"[npiece % 2], x))
+            npiece += 1
+        if e0 == 1024:
+            wait("V", ("gi", 32))
+            vs1 = done("V", g.vector.tensor_copy(T.snd1[:], T.snd1i[:]))
+    for p in pend:
+        evac(p)
+
+    own1 = exchange(T.w1, T.sb1, T.snd1, h0 + [vs1], "arr1")
+
+    vl1 = done("V", g.vector.tensor_copy(T.l1[:], T.l1i[:]))
+    tl32 = done("V", g.vector.tensor_copy(T.l32[:], T.lb[:]))
+    wait("P", taw, tl32)
+    wait("P", *h0)
+    p1 = done("P", g.tensor.matmul(bank(0, 128), T.l32[:], T.awr[:], True, True))
+    p2 = done("P", g.tensor.matmul(bank(1, 1), T.l32[:], T.abt[:], True, True))
+    p3 = done("P", g.tensor.matmul(bank(2, 16), T.l32[:], T.l32[:, 0:16], True, True))
+    wait("V", p1, tbd)
+    tawb = done("V", g.vector.tensor_tensor(T.awb[:], bank(0, 128), T.bd[:], A.mult))
+    wait("V", p2)
+    tabc = done("V", g.vector.tensor_copy(T.abc[:], bank(1, 1)))
+    wait("V", p3)
+    td16 = done("V", g.vector.tensor_copy(T.d16[:], bank(2, 16)))
+    wait("V", tql)
+    qs = (T.q0, T.q1, T.q2, T.q3)
+    for q in range(N):
+        tq = done("V", g.vector.tensor_scalar(qs[q][:], T.bd[:], T.aqs[:, 4 * q:4 * q + 1], 2.0 ** -14, A.mult, A.mult))
+
+    ch = [(0, 256), (512, 512), (1024, 512), (1536, 512), (2048, 512), (2560, 512), (3072, 512), (3584, 256), (3840, 256),
+          (256, 256)]
+    nch = len(ch)
+    arrived = [("arr1", 3 * eng), own1, vl1] + h0
+    tg, ts, th, tt = [None] * nch, [None] * nch, [None] * nch, [None] * nch
+    NB = 6
+
+    def off(j, d):
+        e0, n = ch[j]
+        return T.l1[:, 256 * d + e0 // 16:256 * d + (e0 + n) // 16]
+
+    def first(j):
+        e0, n = ch[j]
+        tg[j] = gather("S", T.a0[:, e0:e0 + n], T.w1[:], off(j, 0), arrived)
+
+    def add(j, d):
+        e0, n = ch[j]
+        src, dst = (T.a0, T.a1) if d % 2 else (T.a1, T.a0)
+        wait("V", tg[j] if d == 1 else ts[j], *arrived)
+        ts[j] = done("V", g.vector.tensor_tensor(dst[:, e0:e0 + n], T.w1[:].indirect(off(j, d)), src[:, e0:e0 + n], A.add))
+
+    def hview(j):
+        e0, n = ch[j]
+        return T.h[:, e0:e0 + n]
+
+    def relu(q, j):
+        e0, n = ch[j]
+        i = T.a1[:, e0:e0 + n]
+        wait(q, ts[j], tb1)
+        if q == "V":
+            th[j] = done("V", g.vector.tensor_scalar(hview(j), i, T.b1[:], 0.0, A.add, A.max))
+        else:
+            th[j] = done("S", g.scalar.activation(hview(j), i, F.Relu, bias=T.b1[:]))
+        wait("P", tawb, tabc, td16, th[j])
+        if j >= NB:
+            wait("P", tt[j - NB])
+        tt[j] = done("P", g.tensor.matmul(bank(j % NB, n), T.awb[:], hview(j), True, True))
+
+    def tanh(j):
+        e0, n = ch[j]
+        wait("S", tt[j], tabc)
+        tt[j] = done("S", g.scalar.activation(T.th[:, e0:e0 + n], bank(j % NB, n), F.Tanh, bias=T.abc[:],
+                                              accum_out=T.acc[:, 12 * r + j:12 * r + j + 1]))
+
+    def adds(k):
+        for d in (1, 2, 3):
+            for j in (2 * k, 2 * k + 1):
+                add(j, d)
+
+    for j in range(4):
+        first(j)
+    for k in range(nch // 2):
+        adds(k)
+        relu("S", 2 * k)
+        relu("V" if k == nch // 2 - 1 else "S", 2 * k + 1)
+        for j in (2 * k + 4, 2 * k + 5):
+            if j < nch:
+                first(j)
+        tanh(2 * k)
+        tanh(2 * k + 1)
+
+    last = tt[nch - 1]
+    wait("G", last)
+    mine = T.acc[:, 12 * r:12 * r + nch]
+    send_all(mine, mine, "sca")
+    wait("P", last, tq)
+    p1 = done("P", g.tensor.matmul(bank(6, nch), qs[r][:], mine, True, True))
+    wait("P", ("sca", 3 * eng))
+    for i, q in enumerate(ranks):
+        p2 = done("P", g.tensor.matmul(bank(7, nch), qs[q][:], T.acc[:, 12 * q:12 * q + nch], i == 0, i == 2))
+    wait("V", p1)
+    t = done("V", g.vector.tensor_reduce(T.so[:], bank(6, nch), AxisListType.X, A.add))
+    wait("S", t)
+    teo = done("S", g.scalar.activation(T.eo[:], T.so[:], F.Exp))
+    wait("V", p2)
+    t = done("V", g.vector.tensor_reduce(T.st[:], bank(7, nch), AxisListType.X, A.add))
+    wait("S", t)
+    tet = done("S", g.scalar.activation(T.et[:], T.st[:], F.Exp))
+    wait("V", tet, teo)
+    twm = done("V", g.vector.tensor_scalar(T.wm[:], T.d16[:], T.et[:], T.eo[:], A.mult, A.mult))
+    twv = done("V", g.vector.tensor_tensor(T.wv[:], T.et[:], T.eo[:], A.mult))
+
+    wait("P", twm)
+    tz = []
+    for hb in (0, 1):
+        for b in range(8):
+            if hb:
+                wait("P", tz[b])
+            for k in (0, 1):
+                c0 = 1024 * (2 * hb + k)
+                py = done("P", g.tensor.matmul(bank(b, 16, 16 * k), T.h[:, c0 + b:c0 + 1024:8], T.wm[:], True, True))
+            wait("V", py)
+            ty = done("V", g.vector.transpose(T.yt[:, 256 * hb + b:256 * hb + 256:8], bank(b, 32)))
+            tz.append(ty)
+        for a in range(4):
+            for k in (0, 1):
+                q = "YS"[k]
+                wait(q, ty)
+                c0 = 1024 * (2 * hb + k) + 256 * a
+                dma(q, "st%d" % hb, T.y[:, c0:c0 + 256], T.yt[32 * a + 16 * k:32 * a + 16 * k + 16, 256 * hb:256 * hb + 256])
+    wait("Y", twv)
+    dma("Y", "dw", T.w[:], T.wv[0:128:16, :])
+
+    wait("G", ("loc", nloc[0]), ("gi", 32), *total.items())
+    wait("G", *[("c" + q, n) for q, n in cnt.items()])

@@ -3,6 +3,7 @@ from concourse.mybir import AluOpType, AxisListType, ActivationFunctionType
 
 E, CAP, N = 4096, 256, 4
 P = E + N * CAP
+XP = 3072
 SCRATCH = {"aqd": ("dram", [128, 1], "float32"), "aql": ("dram", [4, 128, 1], "float32"),
            "ps": ("psum", [128, 4096], "float32")}
 for _rows, _cols, _dt, _names in (
@@ -10,15 +11,16 @@ for _rows, _cols, _dt, _names in (
         (16, 128, "float32", "l32 awr"), (128, 128, "float32", "cn ones bda bd perm0 perm1 awb q0 q1 q2 q3"),
         (128, 1, "int32", "pio pm"), (128, 1, "float32", "pmf bst b0 b1 abc so st eo et wv"), (8, 2, "int32", "mpi"),
         (8, 2, "bfloat16", "mpf"), (8, 2, "float32", "mpg"), (128, 2, "int32", "idx"), (16, 1, "float32", "abt"),
-        (16, E, "bfloat16", "xs"), (128, 64, "int32", "snd0i snd1i"), (128, 64, "uint16", "snd0 snd1"),
-        (128, 1024, "int32", "l0i l1i"), (128, 1024, "uint16", "l0 l1"), (128, P, "bfloat16", "w0"), (128, P, "float32", "w1"),
-        (128, 3 * CAP, "bfloat16", "sb0"), (128, 3 * CAP, "float32", "sb1"), (128, E, "bfloat16", "ga gb gg gd th"),
-        (128, E, "float32", "a0 a1 h"), (128, 48, "float32", "acc"), (128, 16, "float32", "aqs d16 wm"),
+        (16, 4, "float32", "aq16"), (16, XP, "bfloat16", "xs"), (128, 64, "int32", "snd0i snd1i"),
+        (128, 64, "uint16", "snd0 snd1"), (128, 1024, "int32", "l0i l1i"), (128, 1024, "uint16", "l0 l1"),
+        (128, P, "bfloat16", "w0"), (128, P, "float32", "w1"), (128, 3 * CAP, "bfloat16", "sb0"),
+        (128, 3 * CAP, "float32", "sb1"), (128, E, "bfloat16", "ga gb gg gd th"), (128, E, "float32", "a0 a1 h"),
+        (128, 48, "float32", "acc"), (128, 16, "float32", "ld ldo wm"), (128, 4, "float32", "aqs"),
         (128, 512, "float32", "yt")):
     for _n in _names.split():
         SCRATCH[_n] = ("sbuf", [_rows, _cols], _dt)
-SEMAPHORES = ["cV", "cS", "cP", "cG", "dx", "dsnd", "dmp", "dsrc", "daq", "dbs", "daw", "dql", "gi", "st0", "st1", "dw",
-              "aqa", "arr0", "arr1", "sca", "loc"]
+SEMAPHORES = ["cV", "cS", "cP", "cG", "dx", "dx2", "dxr", "dsnd", "dmp", "dsrc", "daq", "dbs", "daw", "dql", "gi", "st0",
+              "st1", "dw", "aqa", "arr0", "arr1", "sca", "loc"]
 
 
 def rank_program(g, core, T, topo):
@@ -76,11 +78,13 @@ def rank_program(g, core, T, topo):
             return done("V", g.vector.tensor_copy(out, win.indirect(off)))
         return done("S", g.scalar.activation(out, win.indirect(off), F.Identity))
 
-    tx = dma("Y", "dx", T.xs[:], T.x[:])
-    tsnd = dma("S", "dsnd", T.snd0i[:], T.snd[:])
+    tx = [dma("Y", "dx", T.xs[:, 0:XP // 2], T.x[:, 0:XP // 2]), dma("Y", "dx2", T.xs[:, XP // 2:XP], T.x[:, XP // 2:XP])]
+    dma("S", "daq", T.aqd[0:16, :], T.aq[:])
+    taq = dma("S", "daq", T.aqd[16:128, :], T.bs[16:128, :])
+    tsnd = dma("Y", "dsnd", T.snd0i[:], T.snd[:])
     tmp = dma("S", "dmp", T.mpi[:], T.mp[:])
     for k in range(8):
-        taq = dma("S", "daq", T.aqd[16 * k:16 * k + 16, :], T.aq[:])
+        txr = dma("YS"[k % 2], "dxr", T.w0[16 * k:16 * k + 16, XP:E], T.x[:, XP:E])
     tsrc = dma("Y", "dsrc", T.l0i[:], T.src[:])
     tbs = dma("Y", "dbs", T.bst[:], T.bs[:])
     dma("Y", "daw", T.abt[:], T.ab[:])
@@ -97,20 +101,19 @@ def rank_program(g, core, T, topo):
     wait("G", t)
     tr16 = done("G", g.affine_select(T.r16[:], T.r16a[:], [[-1, 128]], A.is_ge, 0.0, 15, 16))
     tpio = done("G", g.iota(T.pio[:], [[0, 1]], 0, 1))
+    tcn = done("G", g.iota(T.cn[:], [[0, 8], [-1, 16]], 0, 1, allow_small_or_imprecise_dtypes=True))
     wait("G", taq)
     send_all(T.aql[r], T.aqd[:], "aqa")
-    tcn = done("G", g.iota(T.cn[:], [[0, 8], [-1, 16]], 0, 1, allow_small_or_imprecise_dtypes=True))
-    wait("G", v3)
-    t = done("G", g.affine_select(T.bda[:], T.ones[:], [[-16, 8], [0, 16]], A.is_ge, 0.0, 0, 1))
-    wait("G", t)
-    tbd = done("G", g.affine_select(T.bd[:], T.bda[:], [[16, 8], [0, 16]], A.is_ge, 0.0, 15, -1))
 
-    wait("P", tlb, tx)
-    px = [done("P", g.tensor.matmul(bank(b, 512), T.lb[:], T.xs[:, 512 * b:512 * b + 512], True, True)) for b in range(8)]
+    wait("P", tlb)
+    px = []
+    for b in range(XP // 512):
+        wait("P", tx[512 * b >= XP // 2])
+        px.append(done("P", g.tensor.matmul(bank(b, 512), T.lb[:], T.xs[:, 512 * b:512 * b + 512], True, True)))
     wait("V", tsnd)
     vsnd = done("V", g.vector.tensor_copy(T.snd0[:], T.snd0i[:]))
     xe = []
-    for b in range(8):
+    for b in range(XP // 512):
         q = "VS"[b % 2]
         wait(q, px[b])
         o = T.w0[:, 512 * b:512 * b + 512]
@@ -122,19 +125,19 @@ def rank_program(g, core, T, topo):
     def exchange(win, sb, lists, deps, sem):
         w = win[:, 0:E]
         tk = []
-        for i, q in ((0, "V"), (1, "S"), (2, "V")):
-            off = lists[:, 16 * ranks[i]:16 * ranks[i] + 16]
-            tk.append(gather(q, sb[:, CAP * i:CAP * i + CAP], w, off, deps))
+        for i, q, o, n in ((0, "V", 0, 128), (0, "S", 128, 128), (1, "V", 0, 256), (2, "S", 0, 256)):
+            c0 = 16 * ranks[i] + o // 16
+            tk.append((i, gather(q, sb[:, CAP * i + o:CAP * i + o + n], w, lists[:, c0:c0 + n // 16], deps)))
         own = gather("S", win[:, E + CAP * r:E + CAP * r + CAP], w, lists[:, 16 * r:16 * r + 16], deps)
         for i in range(3):
-            wait("G", tk[i])
+            wait("G", *[t for j, t in tk if j == i])
             send(win[:, E + CAP * r:E + CAP * r + CAP], sb[:, CAP * i:CAP * i + CAP], sem, peers[i])
         return own
 
-    own0 = exchange(T.w0, T.sb0, T.snd0, xe + [vsnd], "arr0")
+    own0 = exchange(T.w0, T.sb0, T.snd0, xe + [vsnd, txr], "arr0")
 
     wait("V", tmp)
-    t = done("V", g.vector.tensor_copy(T.mpf[:], T.mpi[:]))
+    done("V", g.vector.tensor_copy(T.mpf[:], T.mpi[:]))
     t3 = done("V", g.vector.tensor_copy(T.mpg[:], T.mpi[:]))
     wait("V", tpio)
     t2 = done("V", g.vector.tensor_scalar(T.pm[:], T.pio[:], 15, None, A.bitwise_and))
@@ -146,33 +149,36 @@ def rank_program(g, core, T, topo):
     wait("P", tr16, *tm)
     wait("P", *xe)
     pidx = done("P", g.tensor.matmul(bank(2, 2), T.r16[:], T.mpf[:], True, True))
-    pa = [done("P", g.tensor.matmul(bank(s, 128), (T.mpr0, T.mpr1)[s][:], T.r16[:], True, True)) for s in (0, 1)]
+    pa = done("P", g.tensor.matmul(bank(0, 128), T.mpr0[:], T.r16[:], True, True))
     wait("V", pidx, tpm)
     tidx = done("V", g.vector.tensor_scalar(T.idx[:], bank(2, 2), T.pmf[:], None, A.add))
-    wait("V", tcn, *pa)
-    tp = [done("V", g.vector.tensor_tensor((T.perm0, T.perm1)[s][:], bank(s, 128), T.cn[:], A.is_equal)) for s in (0, 1)]
+    wait("V", tcn, pa)
+    t = done("V", g.vector.tensor_tensor(T.perm0[:], bank(0, 128), T.cn[:], A.is_equal))
     wait("V", tsrc)
     vl0 = done("V", g.vector.tensor_copy(T.l0[:], T.l0i[:]))
-    wait("V", tp[0])
-    tpb = done("V", g.vector.tensor_scalar(T.permb[:], T.perm0[:], 0.0625, None, A.mult))
-    wait("P", tbs, *tp)
-    pb = [done("P", g.tensor.matmul(bank(3 + s, 1), (T.perm0, T.perm1)[s][:], T.bst[:], True, True)) for s in (0, 1)]
-    wait("V", *pb)
-    tb0 = done("V", g.vector.tensor_scalar(T.b0[:], bank(3, 1), 0.25, None, A.mult))
-    tb1 = done("V", g.vector.tensor_copy(T.b1[:], bank(4, 1)))
+    wait("S", t)
+    tpb = done("S", g.scalar.activation(T.permb[:], T.perm0[:], F.Identity, scale=0.0625))
+    wait("P", tbs, t)
+    t = done("P", g.tensor.matmul(bank(3, 1), T.perm0[:], T.bst[:], True, True))
+    wait("S", t)
+    tb0 = done("S", g.scalar.activation(T.b0[:], bank(3, 1), F.Identity, scale=0.25))
     wait("G", tidx)
     for o, tab in ((T.snd1i, T.snd), (T.l1i, T.src)):
         g.indirect_dma_start(o[:], None, tab[:], IndirectOffsetOnAxis(ap=T.idx[:, 1:2], axis=0),
                              bounds_check=127).then_inc(T.sem.gi, 16)
+    wait("G", v3)
+    t = done("G", g.affine_select(T.bda[:], T.ones[:], [[-16, 8], [0, 16]], A.is_ge, 0.0, 0, 1))
+    wait("G", t)
+    tbd = done("G", g.affine_select(T.bd[:], T.bda[:], [[16, 8], [0, 16]], A.is_ge, 0.0, 15, -1))
     wait("Y", taq)
-    dma("Y", "dql", T.aqs[:, 4 * r:4 * r + 1], T.aqd[:])
+    dma("Y", "dql", T.aq16[:, r:r + 1], T.aqd[0:16, :])
     wait("Y", ("aqa", 3 * eng))
     for q in ranks:
-        tql = dma("Y", "dql", T.aqs[:, 4 * q:4 * q + 1], T.aql[q])
+        tql = dma("Y", "dql", T.aq16[:, q:q + 1], T.aql[q, 0:16, :])
 
     bufs = (T.ga, T.gb, T.gg, T.gd)
-    chunks = [(0, 1024), (1024, 1024), (2048, 1024), (3072, 512), (3584, 256), (3840, 256)]
-    arrived = [("arr0", 3 * eng), own0, vl0] + xe
+    chunks = [(0, 1024), (1024, 1024), (2048, 1024), (3072, 512), (3584, 256), (3840, 128), (3968, 128)]
+    arrived = [("arr0", 3 * eng), own0, vl0, txr] + xe
     pend, h0, npiece = [], [], 0
 
     def evac(p):
@@ -193,7 +199,7 @@ def rank_program(g, core, T, topo):
         for c0 in range(e0, e0 + n, 512):
             m = min(512, e0 + n - c0)
             b = npiece % 8
-            wait("P", tpb, tb0, tb1)
+            wait("P", tpb, tb0)
             if npiece >= 8:
                 wait("P", h0[npiece - 8])
             for i, d in enumerate((0, 2, 1, 3)):
@@ -211,27 +217,38 @@ def rank_program(g, core, T, topo):
 
     vl1 = done("V", g.vector.tensor_copy(T.l1[:], T.l1i[:]))
     tl32 = done("V", g.vector.tensor_copy(T.l32[:], T.lb[:]))
-    wait("P", taw, tl32)
+    wait("P", taw, tql, tl32)
     wait("P", *h0)
     p1 = done("P", g.tensor.matmul(bank(0, 128), T.l32[:], T.awr[:], True, True))
     p2 = done("P", g.tensor.matmul(bank(1, 1), T.l32[:], T.abt[:], True, True))
     p3 = done("P", g.tensor.matmul(bank(2, 16), T.l32[:], T.l32[:, 0:16], True, True))
+    p4 = done("P", g.tensor.matmul(bank(3, 4), T.l32[:], T.aq16[:], True, True))
+    p5 = done("P", g.tensor.matmul(bank(4, 128), T.mpr1[:], T.r16[:], True, True))
+    wait("V", p5)
+    t = done("V", g.vector.tensor_tensor(T.perm1[:], bank(4, 128), T.cn[:], A.is_equal))
+    wait("P", t)
+    p6 = done("P", g.tensor.matmul(bank(5, 1), T.perm1[:], T.bst[:], True, True))
     wait("V", p1, tbd)
     tawb = done("V", g.vector.tensor_tensor(T.awb[:], bank(0, 128), T.bd[:], A.mult))
     wait("V", p2)
     tabc = done("V", g.vector.tensor_copy(T.abc[:], bank(1, 1)))
     wait("V", p3)
-    td16 = done("V", g.vector.tensor_copy(T.d16[:], bank(2, 16)))
-    wait("V", tql)
+    tl = done("V", g.vector.tensor_scalar(T.ld[:], bank(2, 16), -1.0, 1024.0, A.add, A.mult))
+    wait("V", p6)
+    tb1 = done("V", g.vector.tensor_copy(T.b1[:], bank(5, 1)))
+    wait("V", p4)
+    t = done("V", g.vector.tensor_copy(T.aqs[:], bank(3, 4)))
+    wait("V", t)
     qs = (T.q0, T.q1, T.q2, T.q3)
     for q in range(N):
-        tq = done("V", g.vector.tensor_scalar(qs[q][:], T.bd[:], T.aqs[:, 4 * q:4 * q + 1], 2.0 ** -14, A.mult, A.mult))
+        tq = done("V", g.vector.tensor_scalar(qs[q][:], T.bd[:], T.aqs[:, q:q + 1], 2.0 ** -14, A.mult, A.mult))
 
-    ch = [(0, 256), (512, 512), (1024, 512), (1536, 512), (2048, 512), (2560, 512), (3072, 512), (3584, 256), (3840, 256),
-          (256, 256)]
+    ch = [(0, 256), (256, 256), (512, 512), (1024, 512), (1536, 512), (2048, 512), (2560, 512), (3072, 512), (3584, 256),
+          (3840, 128), (3968, 128)]
+    sets = [(0, 1), (2, 3), (4, 5), (6, 7, 8), (9, 10)]
     nch = len(ch)
     arrived = [("arr1", 3 * eng), own1, vl1] + h0
-    tg, ts, th, tt = [None] * nch, [None] * nch, [None] * nch, [None] * nch
+    tg, ts, tt = [None] * nch, [None] * nch, [None] * nch
     NB = 6
 
     def off(j, d):
@@ -248,22 +265,18 @@ def rank_program(g, core, T, topo):
         wait("V", tg[j] if d == 1 else ts[j], *arrived)
         ts[j] = done("V", g.vector.tensor_tensor(dst[:, e0:e0 + n], T.w1[:].indirect(off(j, d)), src[:, e0:e0 + n], A.add))
 
-    def hview(j):
-        e0, n = ch[j]
-        return T.h[:, e0:e0 + n]
-
     def relu(q, j):
         e0, n = ch[j]
-        i = T.a1[:, e0:e0 + n]
+        i, o = T.a1[:, e0:e0 + n], T.h[:, e0:e0 + n]
         wait(q, ts[j], tb1)
         if q == "V":
-            th[j] = done("V", g.vector.tensor_scalar(hview(j), i, T.b1[:], 0.0, A.add, A.max))
+            th = done("V", g.vector.tensor_scalar(o, i, T.b1[:], 0.0, A.add, A.max))
         else:
-            th[j] = done("S", g.scalar.activation(hview(j), i, F.Relu, bias=T.b1[:]))
-        wait("P", tawb, tabc, td16, th[j])
+            th = done("S", g.scalar.activation(o, i, F.Relu, bias=T.b1[:]))
+        wait("P", tawb, tq, th)
         if j >= NB:
             wait("P", tt[j - NB])
-        tt[j] = done("P", g.tensor.matmul(bank(j % NB, n), T.awb[:], hview(j), True, True))
+        tt[j] = done("P", g.tensor.matmul(bank(j % NB, n), T.awb[:], o, True, True))
 
     def tanh(j):
         e0, n = ch[j]
@@ -271,22 +284,18 @@ def rank_program(g, core, T, topo):
         tt[j] = done("S", g.scalar.activation(T.th[:, e0:e0 + n], bank(j % NB, n), F.Tanh, bias=T.abc[:],
                                               accum_out=T.acc[:, 12 * r + j:12 * r + j + 1]))
 
-    def adds(k):
-        for d in (1, 2, 3):
-            for j in (2 * k, 2 * k + 1):
-                add(j, d)
-
-    for j in range(4):
+    for j in sets[0] + sets[1]:
         first(j)
-    for k in range(nch // 2):
-        adds(k)
-        relu("S", 2 * k)
-        relu("V" if k == nch // 2 - 1 else "S", 2 * k + 1)
-        for j in (2 * k + 4, 2 * k + 5):
-            if j < nch:
-                first(j)
-        tanh(2 * k)
-        tanh(2 * k + 1)
+    for k, js in enumerate(sets):
+        for d in (1, 2, 3):
+            for j in js:
+                add(j, d)
+        for j in js:
+            relu("V" if k == len(sets) - 1 else "S", j)
+        for j in (sets[k + 2] if k + 2 < len(sets) else ()):
+            first(j)
+        for j in js:
+            tanh(j)
 
     last = tt[nch - 1]
     wait("G", last)
@@ -301,12 +310,14 @@ def rank_program(g, core, T, topo):
     t = done("V", g.vector.tensor_reduce(T.so[:], bank(6, nch), AxisListType.X, A.add))
     wait("S", t)
     teo = done("S", g.scalar.activation(T.eo[:], T.so[:], F.Exp))
+    wait("V", t, tl)
+    tld = done("V", g.vector.tensor_scalar(T.ldo[:], T.ld[:], T.so[:], None, A.add))
     wait("V", p2)
     t = done("V", g.vector.tensor_reduce(T.st[:], bank(7, nch), AxisListType.X, A.add))
-    wait("S", t)
+    wait("S", t, tld)
+    twm = done("S", g.scalar.activation(T.wm[:], T.ldo[:], F.Exp, bias=T.st[:]))
     tet = done("S", g.scalar.activation(T.et[:], T.st[:], F.Exp))
     wait("V", tet, teo)
-    twm = done("V", g.vector.tensor_scalar(T.wm[:], T.d16[:], T.et[:], T.eo[:], A.mult, A.mult))
     twv = done("V", g.vector.tensor_tensor(T.wv[:], T.et[:], T.eo[:], A.mult))
 
     wait("P", twm)
@@ -327,8 +338,9 @@ def rank_program(g, core, T, topo):
                 wait(q, ty)
                 c0 = 1024 * (2 * hb + k) + 256 * a
                 dma(q, "st%d" % hb, T.y[:, c0:c0 + 256], T.yt[32 * a + 16 * k:32 * a + 16 * k + 16, 256 * hb:256 * hb + 256])
-    wait("Y", twv)
-    dma("Y", "dw", T.w[:], T.wv[0:128:16, :])
+        if hb == 0:
+            wait("Y", twv)
+            dma("Y", "dw", T.w[:], T.wv[0:128:16, :])
 
     wait("G", ("loc", nloc[0]), ("gi", 32), *total.items())
     wait("G", *[("c" + q, n) for q, n in cnt.items()])

@@ -15,12 +15,24 @@ for _rows, _cols, _dt, _names in (
         (128, 64, "uint16", "snd0 snd1"), (128, 1024, "int32", "l0i l1i"), (128, 1024, "uint16", "l0 l1"),
         (128, P, "bfloat16", "w0"), (128, P, "float32", "w1"), (128, 3 * CAP, "bfloat16", "sb0"),
         (128, 3 * CAP, "float32", "sb1"), (128, E, "bfloat16", "ga gb gg gd th"), (128, E, "float32", "a0 a1 h"),
-        (128, 48, "float32", "acc"), (128, 16, "float32", "ld ldo wm"), (128, 4, "float32", "aqs"),
-        (128, 512, "float32", "yt")):
+        (128, 48, "float32", "acc"), (128, 16, "float32", "ld ldo wm"), (128, 16, "bfloat16", "ldb"),
+        (128, 4, "float32", "aqs"), (128, 512, "float32", "yt")):
     for _n in _names.split():
         SCRATCH[_n] = ("sbuf", [_rows, _cols], _dt)
 SEMAPHORES = ["cV", "cS", "cP", "cG", "dx", "dx2", "dxr", "dsnd", "dmp", "dsrc", "daq", "dbs", "daw", "dql", "gi", "st0",
-              "st1", "dw", "aqa", "arr0", "arr1", "sca", "loc"]
+              "st1", "dw", "aqa", "arr0", "arr1", "sca0", "sca1", "sca2", "sca3", "ac5", "ac6", "ac7", "loc"]
+
+CH = [(0, 256), (256, 256), (512, 512), (1024, 512), (1536, 512), (2048, 512), (2560, 512), (3072, 512), (3584, 256),
+      (3840, 128), (3968, 128)]
+TWO = (5, 6, 7)
+ORDER = {
+    "V": "0.0 0.1 2.1 0.2 2.2 1.1 0.3 1.2 3.1 1.3 2.3 1.r 4.1 3.2 4.2 3.3 5.2 4.3 5.3 6.2 8.1 6.3 7.2 9.1 7.3 9.2 8.2 10.1 "
+         "8.3 10.2 8.r 10.3 9.3 10.r 9.r",
+    "S": "2.0 5.0 1.0 3.0 5.1 4.0 6.0 0.r 6.1 2.r 7.1 7.0 0.t 10.0 9.0 3.r 1.t 8.0 4.r 5.r 3.t 2.t 6.r 4.t 7.r 6.t 5.t 7.t "
+         "8.t 10.t 9.t",
+    "P": "0.m 1.m 2.m 3.m 4.m 5.m 6.m 7.m 8.m 10.m 9.m",
+    "G": "5.+ 6.+ 7.+"}
+NB = 6
 
 
 def rank_program(g, core, T, topo):
@@ -215,8 +227,8 @@ def rank_program(g, core, T, topo):
 
     own1 = exchange(T.w1, T.sb1, T.snd1, h0 + [vs1], "arr1")
 
-    vl1 = done("V", g.vector.tensor_copy(T.l1[:], T.l1i[:]))
     tl32 = done("V", g.vector.tensor_copy(T.l32[:], T.lb[:]))
+    vl1 = done("V", g.vector.tensor_copy(T.l1[:], T.l1i[:]))
     wait("P", taw, tql, tl32)
     wait("P", *h0)
     p1 = done("P", g.tensor.matmul(bank(0, 128), T.l32[:], T.awr[:], True, True))
@@ -224,87 +236,87 @@ def rank_program(g, core, T, topo):
     p3 = done("P", g.tensor.matmul(bank(2, 16), T.l32[:], T.l32[:, 0:16], True, True))
     p4 = done("P", g.tensor.matmul(bank(3, 4), T.l32[:], T.aq16[:], True, True))
     p5 = done("P", g.tensor.matmul(bank(4, 128), T.mpr1[:], T.r16[:], True, True))
+    wait("S", p3)
+    tldb = done("S", g.scalar.activation(T.ldb[:], bank(2, 16), F.Tanh, scale=16.0))
     wait("V", p5)
     t = done("V", g.vector.tensor_tensor(T.perm1[:], bank(4, 128), T.cn[:], A.is_equal))
     wait("P", t)
     p6 = done("P", g.tensor.matmul(bank(5, 1), T.perm1[:], T.bst[:], True, True))
+    wait("V", p4)
+    t = done("V", g.vector.tensor_scalar(T.aqs[:], bank(3, 4), 2.0 ** -14, None, A.mult))
     wait("V", p1, tbd)
     tawb = done("V", g.vector.tensor_tensor(T.awb[:], bank(0, 128), T.bd[:], A.mult))
     wait("V", p2)
     tabc = done("V", g.vector.tensor_copy(T.abc[:], bank(1, 1)))
-    wait("V", p3)
-    tl = done("V", g.vector.tensor_scalar(T.ld[:], bank(2, 16), -1.0, 1024.0, A.add, A.mult))
+    wait("V", tldb)
+    tl = done("V", g.vector.tensor_scalar(T.ld[:], T.ldb[:], -1.0, 1024.0, A.add, A.mult))
     wait("V", p6)
     tb1 = done("V", g.vector.tensor_copy(T.b1[:], bank(5, 1)))
-    wait("V", p4)
-    t = done("V", g.vector.tensor_copy(T.aqs[:], bank(3, 4)))
-    wait("V", t)
+    wait("S", t, tbd)
     qs = (T.q0, T.q1, T.q2, T.q3)
     for q in range(N):
-        tq = done("V", g.vector.tensor_scalar(qs[q][:], T.bd[:], T.aqs[:, q:q + 1], 2.0 ** -14, A.mult, A.mult))
+        tq = done("S", g.scalar.activation(qs[q][:], T.bd[:], F.Identity, scale=T.aqs[:, q:q + 1]))
 
-    ch = [(0, 256), (256, 256), (512, 512), (1024, 512), (1536, 512), (2048, 512), (2560, 512), (3072, 512), (3584, 256),
-          (3840, 128), (3968, 128)]
-    sets = [(0, 1), (2, 3), (4, 5), (6, 7, 8), (9, 10)]
-    nch = len(ch)
     arrived = [("arr1", 3 * eng), own1, vl1] + h0
-    tg, ts, tt = [None] * nch, [None] * nch, [None] * nch
-    NB = 6
+    ready = {}
+    pord = [int(x.split(".")[0]) for x in ORDER["P"].split()]
 
-    def off(j, d):
-        e0, n = ch[j]
-        return T.l1[:, 256 * d + e0 // 16:256 * d + (e0 + n) // 16]
+    def needs(j, k):
+        if k == "0" or k == "1" and j in TWO:
+            return []
+        if k == "+":
+            return [(j, "0"), (j, "1")]
+        if k == "m":
+            i = pord.index(j)
+            return [(j, "r")] + ([(pord[i - NB], "t")] if i >= NB else [])
+        before = {"1": "0", "2": "+" if j in TWO else "1", "3": "2", "r": "3", "t": "m"}
+        return [(j, before[k])]
 
-    def first(j):
-        e0, n = ch[j]
-        tg[j] = gather("S", T.a0[:, e0:e0 + n], T.w1[:], off(j, 0), arrived)
+    def emit(q, j, k):
+        e0, n = CH[j]
+        s = slice(e0, e0 + n)
+        wait(q, *[ready[x] for x in needs(j, k)])
+        sums = (T.a0, T.a0, T.a1, T.a0) if j in TWO else (T.a0, T.a1, T.a0, T.a1)
+        if k in "0123":
+            off = T.l1[:, 256 * int(k) + e0 // 16:256 * int(k) + (e0 + n) // 16]
+            if k == "0" or k == "1" and j in TWO:
+                return gather(q, (T.a0 if k == "0" else T.h)[:, s], T.w1[:], off, arrived)
+            wait("V", *arrived)
+            return done("V", g.vector.tensor_tensor(sums[int(k)][:, s], T.w1[:].indirect(off), sums[int(k) - 1][:, s], A.add))
+        if k == "+":
+            sem = "ac%d" % j
+            g.dma_start(T.a0[:, s], T.h[:, s], accum_op=A.add).then_inc(T.sem[sem], 16)
+            total[sem] = 16
+            return (sem, 16)
+        if k == "r":
+            wait(q, tb1)
+            if q == "V":
+                return done("V", g.vector.tensor_scalar(T.h[:, s], sums[3][:, s], T.b1[:], 0.0, A.add, A.max))
+            return done("S", g.scalar.activation(T.h[:, s], sums[3][:, s], F.Relu, bias=T.b1[:]))
+        b = bank(pord.index(j) % NB, n)
+        if k == "m":
+            wait("P", tawb, tb1, tq)
+            return done("P", g.tensor.matmul(b, T.awb[:], T.h[:, s], True, True))
+        wait("S", tabc)
+        return done("S", g.scalar.activation(T.th[:, s], b, F.Tanh, bias=T.abc[:],
+                                             accum_out=T.acc[:, 12 * r + j:12 * r + j + 1]))
 
-    def add(j, d):
-        e0, n = ch[j]
-        src, dst = (T.a0, T.a1) if d % 2 else (T.a1, T.a0)
-        wait("V", tg[j] if d == 1 else ts[j], *arrived)
-        ts[j] = done("V", g.vector.tensor_tensor(dst[:, e0:e0 + n], T.w1[:].indirect(off(j, d)), src[:, e0:e0 + n], A.add))
+    left = {q: [(int(x.split(".")[0]), x.split(".")[1]) for x in ORDER[q].split()] for q in "VSPG"}
+    while any(left.values()):
+        for q in "VSPG":
+            while left[q] and all(x in ready for x in needs(*left[q][0])):
+                x = left[q].pop(0)
+                ready[x] = last = emit(q, *x)
 
-    def relu(q, j):
-        e0, n = ch[j]
-        i, o = T.a1[:, e0:e0 + n], T.h[:, e0:e0 + n]
-        wait(q, ts[j], tb1)
-        if q == "V":
-            th = done("V", g.vector.tensor_scalar(o, i, T.b1[:], 0.0, A.add, A.max))
-        else:
-            th = done("S", g.scalar.activation(o, i, F.Relu, bias=T.b1[:]))
-        wait("P", tawb, tq, th)
-        if j >= NB:
-            wait("P", tt[j - NB])
-        tt[j] = done("P", g.tensor.matmul(bank(j % NB, n), T.awb[:], o, True, True))
-
-    def tanh(j):
-        e0, n = ch[j]
-        wait("S", tt[j], tabc)
-        tt[j] = done("S", g.scalar.activation(T.th[:, e0:e0 + n], bank(j % NB, n), F.Tanh, bias=T.abc[:],
-                                              accum_out=T.acc[:, 12 * r + j:12 * r + j + 1]))
-
-    for j in sets[0] + sets[1]:
-        first(j)
-    for k, js in enumerate(sets):
-        for d in (1, 2, 3):
-            for j in js:
-                add(j, d)
-        for j in js:
-            relu("V" if k == len(sets) - 1 else "S", j)
-        for j in (sets[k + 2] if k + 2 < len(sets) else ()):
-            first(j)
-        for j in js:
-            tanh(j)
-
-    last = tt[nch - 1]
+    nch = len(CH)
+    last = ("cS", cnt["S"])
     wait("G", last)
     mine = T.acc[:, 12 * r:12 * r + nch]
-    send_all(mine, mine, "sca")
+    send_all(mine, mine, "sca%d" % r)
     wait("P", last, tq)
     p1 = done("P", g.tensor.matmul(bank(6, nch), qs[r][:], mine, True, True))
-    wait("P", ("sca", 3 * eng))
-    for i, q in enumerate(ranks):
+    for i, q in enumerate(ranks[::-1]):
+        wait("P", ("sca%d" % q, eng))
         p2 = done("P", g.tensor.matmul(bank(7, nch), qs[q][:], T.acc[:, 12 * q:12 * q + nch], i == 0, i == 2))
     wait("V", p1)
     t = done("V", g.vector.tensor_reduce(T.so[:], bank(6, nch), AxisListType.X, A.add))

from concourse.bass import DstId, RemoteDMATransfer, IndirectOffsetOnAxis
from concourse.mybir import AluOpType, AxisListType, ActivationFunctionType

E, CAP, N = 4096, 256, 4
P = E + N * CAP
XP = 3072
SCRATCH = {"aqd": ("dram", [128, 1], "float32"), "aql": ("dram", [4, 128, 1], "float32"),
           "ps": ("psum", [128, 4096], "float32")}
for _rows, _cols, _dt, _names in (
        (128, 128, "bfloat16", "onesb permb"), (8, 128, "bfloat16", "c16 r16a r16 mpr0 mpr1"), (16, 128, "bfloat16", "lb"),
        (16, 128, "float32", "l32 awr"), (128, 128, "float32", "cn ones bda bd perm0 perm1 awb q0 q1 q2 q3"),
        (128, 1, "int32", "pio pm"), (128, 1, "float32", "pmf bst b0 b1 abc so st eo et wv"), (8, 2, "int32", "mpi"),
        (8, 2, "bfloat16", "mpf"), (8, 2, "float32", "mpg"), (128, 2, "int32", "idx"), (16, 1, "float32", "abt"),
        (16, 4, "float32", "aq16"), (16, XP, "bfloat16", "xs"), (128, 64, "int32", "snd0i snd1i"),
        (128, 64, "uint16", "snd0 snd1"), (128, 1024, "int32", "l0i l1i"), (128, 1024, "uint16", "l0 l1"),
        (128, P, "bfloat16", "w0"), (128, P, "float32", "w1"), (128, 3 * CAP, "bfloat16", "sb0"),
        (128, 3 * CAP, "float32", "sb1"), (128, E, "bfloat16", "ga gb gg gd th"), (128, E, "float32", "a0 a1 h"),
        (128, 48, "float32", "acc"), (128, 16, "float32", "ld ldo wm"), (128, 16, "bfloat16", "ldb"),
        (128, 4, "float32", "aqs"), (128, 512, "float32", "yt")):
    for _n in _names.split():
        SCRATCH[_n] = ("sbuf", [_rows, _cols], _dt)
SEMAPHORES = ["cV", "cS", "cP", "cG", "dx", "dx2", "dxr", "dsnd", "dmp", "dsrc", "daq", "dbs", "daw", "dql", "gi", "st0",
              "st1", "dw", "aqa", "arr0", "arr1", "sca0", "sca1", "sca2", "sca3", "ac5", "ac6", "ac7", "loc"]

CH = [(0, 256), (256, 256), (512, 512), (1024, 512), (1536, 512), (2048, 512), (2560, 512), (3072, 512), (3584, 256),
      (3840, 128), (3968, 128)]
TWO = (5, 6, 7)
ORDER = {
    "V": "0.0 0.1 2.1 0.2 2.2 1.1 0.3 1.2 3.1 1.3 2.3 1.r 4.1 3.2 4.2 3.3 5.2 4.3 5.3 6.2 8.1 6.3 7.2 9.1 7.3 9.2 8.2 10.1 "
         "8.3 10.2 8.r 10.3 9.3 10.r 9.r",
    "S": "2.0 5.0 1.0 3.0 5.1 4.0 6.0 0.r 6.1 2.r 7.1 7.0 0.t 10.0 9.0 3.r 1.t 8.0 4.r 5.r 3.t 2.t 6.r 4.t 7.r 6.t 5.t 7.t "
         "8.t 10.t 9.t",
    "P": "0.m 1.m 2.m 3.m 4.m 5.m 6.m 7.m 8.m 10.m 9.m",
    "G": "5.+ 6.+ 7.+"}
NB = 6


def rank_program(g, core, T, topo):
    r = T.rank_of(core)
    if r is None:
        return
    A, F = AluOpType, ActivationFunctionType
    queues = {"V": g.vector, "S": g.scalar, "P": g.tensor, "G": g, "Y": g.sync}
    cnt = {"V": 0, "S": 0, "P": 0, "G": 0}
    seen = {}
    total = {}

    def wait(q, *tokens):
        for t in tokens:
            s, v = t
            if seen.get((q, s), 0) < v:
                queues[q].wait_ge(T.sem[s], v)
                seen[(q, s)] = v

    def done(q, ins):
        ins.then_inc(T.sem["c" + q], 1)
        cnt[q] += 1
        return ("c" + q, cnt[q])

    def dma(q, sem, out, in_):
        queues[q].dma_start(out, in_).then_inc(T.sem[sem], 16)
        total[sem] = total.get(sem, 0) + 16
        return (sem, total[sem])

    peers = [T.cores[(r + k) % N] for k in (1, 2, 3)]
    ranks = [(r + k) % N for k in (1, 2, 3)]
    eng = len(topo.engines(core, peers[0]))
    nloc = [0]

    def send(out, in_, sem, dst):
        rid, pid = topo.addr(dst, core)
        g.remote_dma(out, in_, T.sem[sem], T.sem.loc, pid, rid, topo.mask(core, dst))
        nloc[0] += len(topo.engines(core, dst))

    def send_all(out, in_, sem):
        ids = []
        for d in peers:
            rid, pid = topo.addr(d, core)
            ids.append(DstId(rid=rid, pnc=pid))
        g.remote_dma_fused([RemoteDMATransfer(dst_ids=ids, dma_engine_mask=topo.mask(core, peers[0]),
                                              remote_sem=T.sem[sem], src=in_, dsts=[out, out, out])], local_sem=T.sem.loc)
        nloc[0] += eng

    def bank(b, n, o=0):
        return T.ps[:, 512 * b + o:512 * b + o + n]

    def gather(q, out, win, off, deps):
        wait(q, *deps)
        if q == "V":
            return done("V", g.vector.tensor_copy(out, win.indirect(off)))
        return done("S", g.scalar.activation(out, win.indirect(off), F.Identity))

    tx = [dma("Y", "dx", T.xs[:, 0:XP // 2], T.x[:, 0:XP // 2]), dma("Y", "dx2", T.xs[:, XP // 2:XP], T.x[:, XP // 2:XP])]
    dma("S", "daq", T.aqd[0:16, :], T.aq[:])
    taq = dma("S", "daq", T.aqd[16:128, :], T.bs[16:128, :])
    tsnd = dma("Y", "dsnd", T.snd0i[:], T.snd[:])
    tmp = dma("S", "dmp", T.mpi[:], T.mp[:])
    for k in range(8):
        txr = dma("YS"[k % 2], "dxr", T.w0[16 * k:16 * k + 16, XP:E], T.x[:, XP:E])
    tsrc = dma("Y", "dsrc", T.l0i[:], T.src[:])
    tbs = dma("Y", "dbs", T.bst[:], T.bs[:])
    dma("Y", "daw", T.abt[:], T.ab[:])
    for k in range(8):
        taw = dma("Y", "daw", T.awr[:, 16 * k:16 * k + 16], T.aw[:])

    v1 = done("V", g.vector.memset(T.onesb[:], 1.0))
    v2 = done("V", g.vector.memset(T.c16[:], 16.0))
    v3 = done("V", g.vector.memset(T.ones[:], 1.0))
    wait("G", v1)
    tlb = done("G", g.affine_select(T.lb[:], T.onesb[0:16, :], [[0, 8], [1, 16]], A.is_equal, 0.0, 0, -1))
    wait("G", v2)
    t = done("G", g.affine_select(T.r16a[:], T.c16[:], [[1, 128]], A.is_ge, 0.0, 0, -16))
    wait("G", t)
    tr16 = done("G", g.affine_select(T.r16[:], T.r16a[:], [[-1, 128]], A.is_ge, 0.0, 15, 16))
    tpio = done("G", g.iota(T.pio[:], [[0, 1]], 0, 1))
    tcn = done("G", g.iota(T.cn[:], [[0, 8], [-1, 16]], 0, 1, allow_small_or_imprecise_dtypes=True))
    wait("G", taq)
    send_all(T.aql[r], T.aqd[:], "aqa")

    wait("P", tlb)
    px = []
    for b in range(XP // 512):
        wait("P", tx[512 * b >= XP // 2])
        px.append(done("P", g.tensor.matmul(bank(b, 512), T.lb[:], T.xs[:, 512 * b:512 * b + 512], True, True)))
    wait("V", tsnd)
    vsnd = done("V", g.vector.tensor_copy(T.snd0[:], T.snd0i[:]))
    xe = []
    for b in range(XP // 512):
        q = "VS"[b % 2]
        wait(q, px[b])
        o = T.w0[:, 512 * b:512 * b + 512]
        if q == "V":
            xe.append(done("V", g.vector.tensor_copy(o, bank(b, 512))))
        else:
            xe.append(done("S", g.scalar.activation(o, bank(b, 512), F.Identity)))

    def exchange(win, sb, lists, deps, sem):
        w = win[:, 0:E]
        tk = []
        for i, q, o, n in ((0, "V", 0, 128), (0, "S", 128, 128), (1, "V", 0, 256), (2, "S", 0, 256)):
            c0 = 16 * ranks[i] + o // 16
            tk.append((i, gather(q, sb[:, CAP * i + o:CAP * i + o + n], w, lists[:, c0:c0 + n // 16], deps)))
        own = gather("S", win[:, E + CAP * r:E + CAP * r + CAP], w, lists[:, 16 * r:16 * r + 16], deps)
        for i in range(3):
            wait("G", *[t for j, t in tk if j == i])
            send(win[:, E + CAP * r:E + CAP * r + CAP], sb[:, CAP * i:CAP * i + CAP], sem, peers[i])
        return own

    own0 = exchange(T.w0, T.sb0, T.snd0, xe + [vsnd, txr], "arr0")

    wait("V", tmp)
    done("V", g.vector.tensor_copy(T.mpf[:], T.mpi[:]))
    t3 = done("V", g.vector.tensor_copy(T.mpg[:], T.mpi[:]))
    wait("V", tpio)
    t2 = done("V", g.vector.tensor_scalar(T.pm[:], T.pio[:], 15, None, A.bitwise_and))
    wait("V", t3)
    tm = [done("V", g.vector.tensor_scalar(T.mpr0[:], T.onesb[0:8, :], T.mpg[:, 0:1], None, A.mult)),
          done("V", g.vector.tensor_scalar(T.mpr1[:], T.onesb[0:8, :], T.mpg[:, 1:2], None, A.mult))]
    wait("V", t2)
    tpm = done("V", g.vector.tensor_copy(T.pmf[:], T.pm[:]))
    wait("P", tr16, *tm)
    wait("P", *xe)
    pidx = done("P", g.tensor.matmul(bank(2, 2), T.r16[:], T.mpf[:], True, True))
    pa = done("P", g.tensor.matmul(bank(0, 128), T.mpr0[:], T.r16[:], True, True))
    wait("V", pidx, tpm)
    tidx = done("V", g.vector.tensor_scalar(T.idx[:], bank(2, 2), T.pmf[:], None, A.add))
    wait("V", tcn, pa)
    t = done("V", g.vector.tensor_tensor(T.perm0[:], bank(0, 128), T.cn[:], A.is_equal))
    wait("V", tsrc)
    vl0 = done("V", g.vector.tensor_copy(T.l0[:], T.l0i[:]))
    wait("S", t)
    tpb = done("S", g.scalar.activation(T.permb[:], T.perm0[:], F.Identity, scale=0.0625))
    wait("P", tbs, t)
    t = done("P", g.tensor.matmul(bank(3, 1), T.perm0[:], T.bst[:], True, True))
    wait("S", t)
    tb0 = done("S", g.scalar.activation(T.b0[:], bank(3, 1), F.Identity, scale=0.25))
    wait("G", tidx)
    for o, tab in ((T.snd1i, T.snd), (T.l1i, T.src)):
        g.indirect_dma_start(o[:], None, tab[:], IndirectOffsetOnAxis(ap=T.idx[:, 1:2], axis=0),
                             bounds_check=127).then_inc(T.sem.gi, 16)
    wait("G", v3)
    t = done("G", g.affine_select(T.bda[:], T.ones[:], [[-16, 8], [0, 16]], A.is_ge, 0.0, 0, 1))
    wait("G", t)
    tbd = done("G", g.affine_select(T.bd[:], T.bda[:], [[16, 8], [0, 16]], A.is_ge, 0.0, 15, -1))
    wait("Y", taq)
    dma("Y", "dql", T.aq16[:, r:r + 1], T.aqd[0:16, :])
    wait("Y", ("aqa", 3 * eng))
    for q in ranks:
        tql = dma("Y", "dql", T.aq16[:, q:q + 1], T.aql[q, 0:16, :])

    bufs = (T.ga, T.gb, T.gg, T.gd)
    chunks = [(0, 1024), (1024, 1024), (2048, 1024), (3072, 512), (3584, 256), (3840, 128), (3968, 128)]
    arrived = [("arr0", 3 * eng), own0, vl0, txr] + xe
    pend, h0, npiece = [], [], 0

    def evac(p):
        e0, n, b, q, tk = p
        o, i = T.w1[:, e0:e0 + n], bank(b, n)
        wait(q, tk, tb0)
        if q == "V":
            h0.append(done("V", g.vector.tensor_scalar(o, i, T.b0[:], 0.0, A.add, A.max)))
        else:
            h0.append(done("S", g.scalar.activation(o, i, F.Relu, bias=T.b0[:])))

    for e0, n in chunks:
        tk = [gather("VVSS"[d], bufs[d][:, e0:e0 + n], T.w0[:],
                     T.l0[:, 256 * d + e0 // 16:256 * d + (e0 + n) // 16], arrived) for d in (0, 2, 1, 3)]
        for p in pend:
            evac(p)
        pend = []
        for c0 in range(e0, e0 + n, 512):
            m = min(512, e0 + n - c0)
            b = npiece % 8
            wait("P", tpb, tb0)
            if npiece >= 8:
                wait("P", h0[npiece - 8])
            for i, d in enumerate((0, 2, 1, 3)):
                wait("P", tk[i])
                x = done("P", g.tensor.matmul(bank(b, m), T.permb[:], bufs[d][:, c0:c0 + m], i == 0, i == 3))
            pend.append((c0, m, b, "VS"[npiece % 2], x))
            npiece += 1
        if e0 == 1024:
            wait("V", ("gi", 32))
            vs1 = done("V", g.vector.tensor_copy(T.snd1[:], T.snd1i[:]))
    for p in pend:
        evac(p)

    own1 = exchange(T.w1, T.sb1, T.snd1, h0 + [vs1], "arr1")

    tl32 = done("V", g.vector.tensor_copy(T.l32[:], T.lb[:]))
    vl1 = done("V", g.vector.tensor_copy(T.l1[:], T.l1i[:]))
    wait("P", taw, tql, tl32)
    wait("P", *h0)
    p1 = done("P", g.tensor.matmul(bank(0, 128), T.l32[:], T.awr[:], True, True))
    p2 = done("P", g.tensor.matmul(bank(1, 1), T.l32[:], T.abt[:], True, True))
    p3 = done("P", g.tensor.matmul(bank(2, 16), T.l32[:], T.l32[:, 0:16], True, True))
    p4 = done("P", g.tensor.matmul(bank(3, 4), T.l32[:], T.aq16[:], True, True))
    p5 = done("P", g.tensor.matmul(bank(4, 128), T.mpr1[:], T.r16[:], True, True))
    wait("S", p3)
    tldb = done("S", g.scalar.activation(T.ldb[:], bank(2, 16), F.Tanh, scale=16.0))
    wait("V", p5)
    t = done("V", g.vector.tensor_tensor(T.perm1[:], bank(4, 128), T.cn[:], A.is_equal))
    wait("P", t)
    p6 = done("P", g.tensor.matmul(bank(5, 1), T.perm1[:], T.bst[:], True, True))
    wait("V", p4)
    t = done("V", g.vector.tensor_scalar(T.aqs[:], bank(3, 4), 2.0 ** -14, None, A.mult))
    wait("V", p1, tbd)
    tawb = done("V", g.vector.tensor_tensor(T.awb[:], bank(0, 128), T.bd[:], A.mult))
    wait("V", p2)
    tabc = done("V", g.vector.tensor_copy(T.abc[:], bank(1, 1)))
    wait("V", tldb)
    tl = done("V", g.vector.tensor_scalar(T.ld[:], T.ldb[:], -1.0, 1024.0, A.add, A.mult))
    wait("V", p6)
    tb1 = done("V", g.vector.tensor_copy(T.b1[:], bank(5, 1)))
    wait("S", t, tbd)
    qs = (T.q0, T.q1, T.q2, T.q3)
    for q in range(N):
        tq = done("S", g.scalar.activation(qs[q][:], T.bd[:], F.Identity, scale=T.aqs[:, q:q + 1]))

    arrived = [("arr1", 3 * eng), own1, vl1] + h0
    ready = {}
    pord = [int(x.split(".")[0]) for x in ORDER["P"].split()]

    def needs(j, k):
        if k == "0" or k == "1" and j in TWO:
            return []
        if k == "+":
            return [(j, "0"), (j, "1")]
        if k == "m":
            i = pord.index(j)
            return [(j, "r")] + ([(pord[i - NB], "t")] if i >= NB else [])
        before = {"1": "0", "2": "+" if j in TWO else "1", "3": "2", "r": "3", "t": "m"}
        return [(j, before[k])]

    def emit(q, j, k):
        e0, n = CH[j]
        s = slice(e0, e0 + n)
        wait(q, *[ready[x] for x in needs(j, k)])
        sums = (T.a0, T.a0, T.a1, T.a0) if j in TWO else (T.a0, T.a1, T.a0, T.a1)
        if k in "0123":
            off = T.l1[:, 256 * int(k) + e0 // 16:256 * int(k) + (e0 + n) // 16]
            if k == "0" or k == "1" and j in TWO:
                return gather(q, (T.a0 if k == "0" else T.h)[:, s], T.w1[:], off, arrived)
            wait("V", *arrived)
            return done("V", g.vector.tensor_tensor(sums[int(k)][:, s], T.w1[:].indirect(off), sums[int(k) - 1][:, s], A.add))
        if k == "+":
            sem = "ac%d" % j
            g.dma_start(T.a0[:, s], T.h[:, s], accum_op=A.add).then_inc(T.sem[sem], 16)
            total[sem] = 16
            return (sem, 16)
        if k == "r":
            wait(q, tb1)
            if q == "V":
                return done("V", g.vector.tensor_scalar(T.h[:, s], sums[3][:, s], T.b1[:], 0.0, A.add, A.max))
            return done("S", g.scalar.activation(T.h[:, s], sums[3][:, s], F.Relu, bias=T.b1[:]))
        b = bank(pord.index(j) % NB, n)
        if k == "m":
            wait("P", tawb, tb1, tq)
            return done("P", g.tensor.matmul(b, T.awb[:], T.h[:, s], True, True))
        wait("S", tabc)
        return done("S", g.scalar.activation(T.th[:, s], b, F.Tanh, bias=T.abc[:],
                                             accum_out=T.acc[:, 12 * r + j:12 * r + j + 1]))

    left = {q: [(int(x.split(".")[0]), x.split(".")[1]) for x in ORDER[q].split()] for q in "VSPG"}
    while any(left.values()):
        for q in "VSPG":
            while left[q] and all(x in ready for x in needs(*left[q][0])):
                x = left[q].pop(0)
                ready[x] = last = emit(q, *x)

    nch = len(CH)
    last = ("cS", cnt["S"])
    wait("G", last)
    mine = T.acc[:, 12 * r:12 * r + nch]
    send_all(mine, mine, "sca%d" % r)
    wait("P", last, tq)
    p1 = done("P", g.tensor.matmul(bank(6, nch), qs[r][:], mine, True, True))
    for i, q in enumerate(ranks[::-1]):
        wait("P", ("sca%d" % q, eng))
        p2 = done("P", g.tensor.matmul(bank(7, nch), qs[q][:], T.acc[:, 12 * q:12 * q + nch], i == 0, i == 2))
    wait("V", p1)
    t = done("V", g.vector.tensor_reduce(T.so[:], bank(6, nch), AxisListType.X, A.add))
    wait("S", t)
    teo = done("S", g.scalar.activation(T.eo[:], T.so[:], F.Exp))
    wait("V", t, tl)
    tld = done("V", g.vector.tensor_scalar(T.ldo[:], T.ld[:], T.so[:], None, A.add))
    wait("V", p2)
    t = done("V", g.vector.tensor_reduce(T.st[:], bank(7, nch), AxisListType.X, A.add))
    wait("S", t, tld)
    twm = done("S", g.scalar.activation(T.wm[:], T.ldo[:], F.Exp, bias=T.st[:]))
    tet = done("S", g.scalar.activation(T.et[:], T.st[:], F.Exp))
    wait("V", tet, teo)
    twv = done("V", g.vector.tensor_tensor(T.wv[:], T.et[:], T.eo[:], A.mult))

    wait("P", twm)
    tz = []
    for hb in (0, 1):
        for b in range(8):
            if hb:
                wait("P", tz[b])
            for k in (0, 1):
                c0 = 1024 * (2 * hb + k)
                py = done("P", g.tensor.matmul(bank(b, 16, 16 * k), T.h[:, c0 + b:c0 + 1024:8], T.wm[:], True, True))
            wait("V", py)
            ty = done("V", g.vector.transpose(T.yt[:, 256 * hb + b:256 * hb + 256:8], bank(b, 32)))
            tz.append(ty)
        for a in range(4):
            for k in (0, 1):
                q = "YS"[k]
                wait(q, ty)
                c0 = 1024 * (2 * hb + k) + 256 * a
                dma(q, "st%d" % hb, T.y[:, c0:c0 + 256], T.yt[32 * a + 16 * k:32 * a + 16 * k + 16, 256 * hb:256 * hb + 256])
        if hb == 0:
            wait("Y", twv)
            dma("Y", "dw", T.w[:], T.wv[0:128:16, :])

    wait("G", ("loc", nloc[0]), ("gi", 32), *total.items())
    wait("G", *[("c" + q, n) for q, n in cnt.items()])
